import numpy as np
import ml_dtypes


def mxq(x, axis, fmt="e4m3"):
    dtype, down = {"e4m3": (ml_dtypes.float8_e4m3fn, 7), "e5m2": (ml_dtypes.float8_e5m2, 14)}[fmt]
    v = np.moveaxis(np.asarray(x, np.float32).astype(ml_dtypes.bfloat16).astype(np.float64), axis, -1)
    blocks = v.reshape(v.shape[:-1] + (-1, 32))
    amax = np.abs(blocks).max(-1, keepdims=True)
    byte = np.maximum(np.where(amax > 0, np.frexp(amax)[1] - 1 + 127, 0) - down, 1)
    scale = np.exp2(byte - 127.0)
    codes = (blocks / scale).astype(np.float32).astype(dtype).astype(np.float64)
    return np.moveaxis((codes * scale).reshape(v.shape), -1, axis)


WIDE = False


def mx_kscale(k):
    if not WIDE:
        return np.ones(k)
    levels = np.array([10, -10, 5, -5, 0])
    if k % 512:
        return np.exp2(np.random.permutation(np.resize(levels, k // 32))).repeat(32)
    a = np.empty((k // 512, 16))
    for p in range(k // 512):
        a[p, :8] = np.random.permutation(np.resize(levels, 8))
        for g in range(8):
            far = levels[np.abs(levels - a[p, g]) >= 10]
            a[p, g + 8] = far[np.random.randint(len(far))]
    return np.exp2(a.ravel()).repeat(32)


BF16 = ml_dtypes.bfloat16


def bf(x):
    return np.asarray(x, np.float32).astype(BF16)


def f64(x):
    return np.asarray(x).astype(np.float64)


E2M1 = np.array([0.0, 0.5, 1.0, 1.5, 2.0, 3.0, 4.0, 6.0, -0.0, -0.5, -1.0, -1.5, -2.0, -3.0, -4.0, -6.0])


def pack_weight(w, fmt):
    k, n = w.shape
    w = f64(bf(w)).reshape(k // 32, 32, n)
    amax = np.abs(w).max(1)
    if fmt == "e4m3":
        byte = np.frexp(amax)[1] - 1 + 127 - 7
    else:
        mant, ex = np.frexp(amax / 6.0)
        byte = np.where(mant > 0.5, ex, ex - 1) + 127
    byte = np.clip(np.where(amax > 0, byte, 1), 1, 254)
    scaled = (w * np.exp2(127.0 - byte)[:, None, :]).reshape(k, n).astype(np.float32)
    by_word = np.ascontiguousarray(scaled.reshape(k // 512, 128, 4, n).transpose(0, 1, 3, 2))
    if fmt == "e4m3":
        words = by_word.astype(ml_dtypes.float8_e4m3fn).view(np.uint8)
    else:
        c = by_word.astype(ml_dtypes.float4_e2m1fn).view(np.uint8) & 0xF
        words = c[..., 0::2] | (c[..., 1::2] << 4)
    return np.ascontiguousarray(words), np.ascontiguousarray(byte.astype(np.uint8).reshape(k // 512, 16, n))


def unpack_weight(words, scales, fmt):
    g, p, n, _ = words.shape
    if fmt == "e4m3":
        vals = np.ascontiguousarray(words).view(ml_dtypes.float8_e4m3fn).astype(np.float64)
    else:
        nib = np.empty((g, p, n, 4), np.uint8)
        nib[..., 0::2] = words & 0xF
        nib[..., 1::2] = words >> 4
        vals = E2M1[nib]
    vals = vals * np.repeat(np.exp2(scales.astype(np.float64) - 127.0), 8, axis=1)[..., None]
    return vals.transpose(0, 1, 3, 2).reshape(g * 512, n)


T, D, F = 1024, 1024, 1024

DIV = 32.0


def draw0():
    s, u = mx_kscale(D), mx_kscale(T)
    x = bf(np.random.standard_normal((T, D)) * s)
    y = bf(np.random.standard_normal((T, D)) * s)
    words, scales = pack_weight(np.random.standard_normal((D, F)) / np.sqrt(D) / s[:, None], "e4m3")
    return {"x": x,
            "y": y,
            "w_words": words,
            "w_scales": scales,
            "b": bf(np.random.standard_normal(F) * 0.2 * np.sqrt(DIV / np.sqrt(T))),
            "p": bf((1.0 + 0.1 * np.random.standard_normal(T)) * u),
            "q": bf((1.0 + 0.1 * np.random.standard_normal(T)) / u)}


def weighted_observables(states, wq, b, weights):
    h = (mxq(f64(states), 1, "e4m3") @ wq) + f64(b)[None, :]
    return f64(weights)[:, None] * np.tanh(h)


def core(x, y, w_words, w_scales, b, p, q):
    wq = unpack_weight(w_words, w_scales, "e4m3")
    fx = weighted_observables(x, wq, b, p)
    fy = weighted_observables(y, wq, b, q)
    return (mxq(fx, 0, "e4m3").T @ mxq(fy, 0, "e4m3")) / DIV


def e4m3fn_bytes(y):
    return np.clip(np.asarray(y, np.float64), -448.0, 448.0).astype(np.float32).astype(ml_dtypes.float8_e4m3fn).view(np.uint8)


def e4m3fn_values(b):
    return np.asarray(b, np.uint8).view(ml_dtypes.float8_e4m3fn).astype(np.float64)


def setup_inputs():
    d = draw0()
    x0 = np.asarray(d['y']).astype(np.float64)
    s = (np.max(np.abs(x0), axis=(0,), keepdims=True) / 448.0).astype(np.float32)
    out = {}
    for k, v in d.items():
        if k == 'y':
            out['y_bytes'] = e4m3fn_bytes(x0 / s.astype(np.float64))
            out['y_scale'] = s
        else:
            out[k] = v
    return out


def reference(x, y_bytes, y_scale, w_words, w_scales, b, p, q):
    return core(x, e4m3fn_values(y_bytes) * y_scale.astype(np.float64), w_words, w_scales, b, p, q)

@@ -1,0 +1,281 @@
+from contextlib import ExitStack
+
+import concourse.mybir as mybir
+from concourse.masks import make_identity
+
+T, D, F = 1024, 1024, 1024
+DIV = 32.0
+FLOPS = 3 * 2 * T * D * F
+
+F32 = mybir.dt.float32
+BF16 = mybir.dt.bfloat16
+U32 = mybir.dt.uint32
+I32 = mybir.dt.int32
+U8 = mybir.dt.uint8
+FP8 = mybir.dt.float8_e4m3fn
+FP8X4 = mybir.dt.float8_e4m3fn_x4
+MULT = mybir.AluOpType.mult
+ADD = mybir.AluOpType.add
+TANH = mybir.ActivationFunctionType.Tanh
+COPY = mybir.ActivationFunctionType.Copy
+
+P = 128
+PACK = 4
+BANK = 512
+HALVES = 2
+FT = F // P
+
+NFILL = 0
+PLAN = "y00By10A y20By30A y40By50A y60By70A y01By11A y21By31A y41By51A y61By71A x00Bx01A x10Bx11A x20Bx21A x30Bx31A x40Bx41A x50Bx51A x60Bx61A x70Bx71A"
+PREP = {("y", 0): (-5, -4, -3, -2), ("y", 1): (-1, 0, 1, 1), ("x", 0): (2,2,3,3),  ("x", 1): (4,4,5,6)}
+S2LAG = 3
+LOADS = "s y0 b y1 w q B x0 p x1"
+DVE_EVAC = 1
+
+
+def tile_extendeddmdkoopmancrossmoment_w8_kernel(tc, x, y_bytes, y_scale, w_words, w_scales, b, p, q, out):
+    nc = tc.nc
+    with ExitStack() as ctx:
+        keep = ctx.enter_context(tc.tile_pool(name="keep", bufs=1))
+        flow = ctx.enter_context(tc.tile_pool(name="flow", bufs=4))
+        psum = ctx.enter_context(tc.psum_pool(name="psum", bufs=8))
+        ctx.enter_context(tc.manual_schedule())
+
+        def kept(name, shape, dtype):
+            return keep.tile(shape, dtype, name=name, align_bytes=64)
+
+        def new_bank():
+            return psum.tile([P, BANK], F32, name="bank")
+
+        ident = kept("ident", [P, P], F32)
+        ysc_col = kept("ysc_col", [P, 8], F32)
+        ysc_all = kept("ysc_all", [P, D], F32)
+        b_rows = kept("b_rows", [8, P], BF16)
+        b_pad = kept("b_pad", [P, P], F32)
+        b_col = kept("b_col", [P, FT], F32)
+        b_all = kept("b_all", [P, F], BF16)
+        wt = {"x": kept("p_col", [P, HALVES, 16], BF16), "y": kept("q_col", [P, HALVES, 16], BF16)}
+        w_codes = [kept("w_codes%d" % g, [P, F], U32) for g in range(2)]
+        w_scale = kept("w_scale", [P, 2 * F], U8)
+        y_raw = {(h, v): kept("y_raw%d%d" % (h, v), [P, 2 * D], U8) for h in range(2) for v in range(2)}
+        rows = {(s, h, u): kept("rows_%s%d%d" % (s, h, u), [P, D // 2], F32) for s in "xy" for h in range(2) for u in range(4)}
+        turned = {(s, h): kept("turned_%s%d" % (s, h), [P, 2 * BANK * 2], F32) for s in "xy" for h in range(2)}
+        in_codes = {(s, h, g): kept("in_codes_%s%d%d" % (s, h, g), [P, BANK], U32) for s in "xy" for h in range(2) for g in range(2)}
+        in_scale = {(s, h, g): kept("in_scale_%s%d%d" % (s, h, g), [P, BANK], U8) for s in "xy" for h in range(2) for g in range(2)}
+        fy = {(h, c): kept("fy%d%d" % (h, c), [P, BANK * PACK], BF16) for h in range(2) for c in range(2)}
+        fy_codes = {k: kept("fy_codes%d%d" % k, [P, BANK], U32) for k in fy}
+        fy_scale = {k: kept("fy_scale%d%d" % k, [P, BANK], U8) for k in fy}
+        fx = {i: kept("fx%d" % i, [P, 2 * P * PACK], BF16) for i in range(FT)}
+        fx_codes = {i: kept("fx_codes%d" % i, [P, 2 * P], U32) for i in range(FT)}
+        fx_scale = {i: kept("fx_scale%d" % i, [P, 2 * P], U8) for i in range(FT)}
+
+        x_v = x.rearrange("(h m u) d -> h u m d", h=2, u=4)
+        y_v = y_bytes.rearrange("(h m v e) d -> h v m (e d)", h=2, v=2, e=2)
+
+        def load_x(h):
+            for u in range(4):
+                nc.sync.dma_start(out=rows["x", h, u][:], in_=x_v[h][u].bitcast(F32))
+
+        def load_y(h):
+            for v in range(2):
+                nc.sync.dma_start(out=y_raw[h, v][:], in_=y_v[h][v])
+
+        def load_w():
+            for g in range(2):
+                nc.sync.dma_start(out=w_codes[g][:].bitcast(I32), in_=w_words[g].rearrange("p n t -> p (n t)").bitcast(I32))
+            for quad in range(4):
+                nc.sync.dma_start(
+                    out=w_scale[32 * quad : 32 * quad + 4, :].bitcast(I32).rearrange("r (g n) -> r g n", g=2),
+                    in_=w_scales[:, 4 * quad : 4 * quad + 4, :].bitcast(I32).rearrange("g r n -> r g n"),
+                )
+
+        def load_wt(s, vec):
+            nc.sync.dma_start(out=wt[s][:, :, 0:4], in_=vec.rearrange("(h m u) -> m h u", h=2, u=4))
+
+        nc.vector.memset(w_scale[:].bitcast(I32), 0)
+        make_identity(nc, ident[:])
+        for item in LOADS.split():
+            if item == "s":
+                nc.sync.dma_start(out=ysc_col[:], in_=y_scale.rearrange("o (m c) -> (o m) c", c=8))
+            if item == "b":
+                nc.sync.dma_start(out=b_rows[:], in_=b.rearrange("(c m) -> c m", m=P))
+            if item == "B":
+                nc.sync.dma_start(out=b_all[:], in_=b.partition_broadcast(P))
+            if item == "w":
+                load_w()
+            if item == "p":
+                load_wt("x", p)
+            if item == "q":
+                load_wt("y", q)
+            if item[0] == "x":
+                load_x(int(item[1]))
+            if item[0] == "y":
+                load_y(int(item[1]))
+
+        nc.scalar.activation(out=b_pad[:], in_=ident[:], func=TANH)
+        for half in range(2):
+            bank = new_bank()
+            for c in range(4):
+                nc.tensor.transpose(bank[:, c * P : (c + 1) * P], ysc_col[:, 4 * half + c : 4 * half + c + 1].to_broadcast([P, P]), ident[:])
+            dst = ysc_all[:].rearrange("p (m c) -> p m c", c=8)[:, :, 4 * half : 4 * half + 4]
+            src = bank[:].rearrange("p (c m) -> p m c", c=4)
+            if half == 0:
+                nc.scalar.copy(out=dst, in_=src)
+            else:
+                nc.vector.tensor_copy(out=dst, in_=src)
+        nc.scalar.copy(out=b_pad[0:8, :], in_=b_rows[:])
+        bank = new_bank()
+        nc.tensor.transpose(bank[:, 0:P], b_pad[:], ident[:])
+        nc.scalar.copy(out=b_col[:], in_=bank[:, 0:FT])
+
+        held = {}
+
+        def prep(stage, s, h, u):
+            if stage == 0 and s == "y":
+                raw = y_raw[h, u // 2][:, (u % 2) * D : (u % 2 + 1) * D]
+                nc.vector.tensor_tensor(out=rows[s, h, u][:].bitcast(BF16), in0=raw.bitcast(FP8), in1=ysc_all[:], op=MULT)
+            if stage == 1:
+                bank = new_bank()
+                held["prep", s, h, u] = bank
+                for g in range(2):
+                    for e in range(2):
+                        k = 2 * g + e
+                        nc.tensor.transpose(bank[:, k * P : (k + 1) * P], rows[s, h, u][:, 256 * g + e : 256 * (g + 1) : 2], ident[:])
+            if stage == 2:
+                dst = turned[s, h][:].rearrange("p (g t e) -> p g t e", g=2, e=2)[:, :, u * P : (u + 1) * P, :]
+                nc.scalar.copy(out=dst, in_=held["prep", s, h, u][:].rearrange("p (g e t) -> p g t e", g=2, e=2))
+            if stage == 3 and u == 3:
+                for g in range(2):
+                    nc.vector.quantize_mx(
+                        out=in_codes[s, h, g][:].bitcast(FP8X4),
+                        scales=in_scale[s, h, g][:],
+                        in_=turned[s, h][:, g * 1024 : (g + 1) * 1024].bitcast(BF16),
+                    )
+
+        def dest(s, f, h):
+            if s == "y":
+                return fy[h, f // 4][:, (f % 4) * BANK : (f % 4 + 1) * BANK]
+            return fx[f][:, h * BANK : (h + 1) * BANK]
+
+        def unit(stage, s, f, h, route):
+            key = (s, f, h)
+            cols = slice(f * P, (f + 1) * P)
+            weight = wt[s][:, h, 0:4].unsqueeze(1).to_broadcast([P, P, PACK])
+            if stage == 0:
+                bank = new_bank()
+                held[key] = bank
+                if route == "A":
+                    for g in range(2):
+                        nc.tensor.matmul_mx(
+                            out=bank[:],
+                            lhsT=w_codes[g][:, cols].bitcast(FP8X4),
+                            lhsT_scale=w_scale[:, g * F + f * P : g * F + (f + 1) * P],
+                            rhs=in_codes[s, h, g][:].bitcast(FP8X4),
+                            rhs_scale=in_scale[s, h, g][:],
+                            start=(g == 0),
+                            stop=(g == 1),
+                        )
+                else:
+                    for u in range(4):
+                        us = slice(u * P, (u + 1) * P)
+                        for g in range(2):
+                            nc.tensor.matmul_mx(
+                                out=bank[:, us],
+                                lhsT=in_codes[s, h, g][:, us].bitcast(FP8X4),
+                                lhsT_scale=in_scale[s, h, g][:, us],
+                                rhs=w_codes[g][:, cols].bitcast(FP8X4),
+                                rhs_scale=w_scale[:, g * F + f * P : g * F + (f + 1) * P],
+                                start=(g == 0),
+                                stop=(g == 1),
+                            )
+            if stage == 1:
+                mid = flow.tile([P, BANK], F32, name="mid")
+                if route == "A":
+                    nc.scalar.activation(out=mid[:], in_=held[key][:], func=TANH, bias=b_col[:, f : f + 1])
+                else:
+                    nc.vector.tensor_tensor(
+                        out=mid[:].rearrange("p (f u) -> p f u", u=4),
+                        in0=held[key][:].rearrange("p (u f) -> p f u", u=4),
+                        in1=b_all[:, cols].unsqueeze(2).to_broadcast([P, P, PACK]),
+                        op=ADD,
+                    )
+                held[key] = mid
+            if stage == 2:
+                if route == "A":
+                    bank = new_bank()
+                    for u in range(4):
+                        nc.tensor.transpose(bank[:, u * P : (u + 1) * P], held[key][:, u * P : (u + 1) * P], ident[:])
+                    held[key] = bank[:].rearrange("p (u f) -> p f u", u=4)
+                else:
+                    act = flow.tile([P, BANK], F32, name="act")
+                    nc.scalar.activation(out=act[:], in_=held[key][:], func=TANH)
+                    held[key] = act[:].rearrange("p (f u) -> p f u", u=4)
+            if stage == 3:
+                nc.vector.tensor_tensor(out=dest(s, f, h).rearrange("p (f u) -> p f u", u=4), in0=held[key], in1=weight, op=MULT)
+            if stage == 4:
+                if s == "y" and f % 4 == 3:
+                    k = (h, f // 4)
+                    nc.vector.quantize_mx(out=fy_codes[k][:].bitcast(FP8X4), scales=fy_scale[k][:], in_=fy[k][:])
+                if s == "x" and h == 1:
+                    nc.vector.quantize_mx(out=fx_codes[f][:].bitcast(FP8X4), scales=fx_scale[f][:], in_=fx[f][:])
+            if stage == 5 and s == "x" and h == 1:
+                for c in range(2):
+                    bank = new_bank()
+                    held[key, c] = bank
+                    for hh in range(2):
+                        hs = slice(hh * P, (hh + 1) * P)
+                        nc.tensor.matmul_mx(
+                            out=bank[:],
+                            lhsT=fx_codes[f][:, hs].bitcast(FP8X4),
+                            lhsT_scale=fx_scale[f][:, hs],
+                            rhs=fy_codes[hh, c][:].bitcast(FP8X4),
+                            rhs_scale=fy_scale[hh, c][:],
+                            start=(hh == 0),
+                            stop=(hh == 1),
+                        )
+            if stage == 6 and s == "x" and h == 1:
+                for c in range(2):
+                    res = flow.tile([P, BANK], F32, name="res", bufs=8)
+                    if c == 1 and f >= FT - DVE_EVAC:
+                        nc.vector.tensor_scalar(out=res[:], in0=held[key, c][:], scalar1=1.0 / DIV, scalar2=None, op0=MULT)
+                    else:
+                        nc.scalar.activation(out=res[:], in_=held[key, c][:], func=COPY, scale=1.0 / DIV)
+                    nc.sync.dma_start(out=out[cols, c * BANK : (c + 1) * BANK], in_=res[:])
+
+        ticks = []
+        for word in PLAN.split():
+            ticks.append([(word[k], int(word[k + 1]), int(word[k + 2]), word[k + 3]) for k in range(0, len(word), 4)])
+        def at(k):
+            return ticks[k] if 0 <= k < len(ticks) else []
+        def preps(k):
+            return [(s, h, u) for (s, h), t0 in PREP.items() for u in range(4) if t0[u] == k]
+        for k in range(-8, len(ticks) + 3):
+            for un in at(k):
+                unit(0, *un)
+            for un in at(k - S2LAG):
+                unit(5, *un)
+            for un in at(k - 1):
+                if un[3] == "B":
+                    unit(2, *un)
+            for un in at(k):
+                unit(1, *un)
+            for un in at(k - S2LAG):
+                unit(6, *un)
+            if S2LAG == 3:
+                for un in at(k - 2):
+                    unit(4, *un)
+            for pr in preps(k - 1):
+                prep(3, *pr)
+            for pr in preps(k + 1):
+                prep(0, *pr)
+            for un in at(k - 1):
+                if un[3] == "A":
+                    unit(2, *un)
+            for pr in preps(k):
+                prep(1, *pr)
+                prep(2, *pr)
+            for un in at(k - 1):
+                unit(3, *un)
+            if S2LAG == 2:
+                for un in at(k - 1):
+                    unit(4, *un)

@@ -26,10 +26,17 @@ HALVES = 2
 FT = F // P
 
 NFILL = 0
-PLAN = "y00By10A y20By30A y40By50A y60By70A y01By11A y21By31A y41By51A y61By71A x00Bx01A x10Bx11A x20Bx21A x30Bx31A x40Bx41A x50Bx51A x60Bx61A x70Bx71A"
-PREP = {("y", 0): (-5, -4, -3, -2), ("y", 1): (-1, 0, 1, 1), ("x", 0): (2,2,3,3),  ("x", 1): (4,4,5,6)}
+PLAN = "y00Cy10C y20Cy30C y40By50C y60By70C y01By11C y21By31C y41By51C y61Cy71C x00Ax01A x10Bx11A x20Bx21A x30Bx31B x40Bx41B x50Bx51B x60Bx61A x70Ax71A"
+TURN = {('y', 1): (1, 1, 2, 2), ('x', 0): (0, 0, 3, 3), ('x', 1): (4, 4, 5, 5)}
+YMUL = (0, 0, 0, 0)
+YHEAD = 1
+SPLIT = 0
+QDMA = 1
+QSP = (0, 2)
+QAT = 3
+EARLY = 2
 S2LAG = 3
-LOADS = "s y0 b y1 w q B x0 p x1"
+LOADS = "s b y0 w0 y1 S w1 Q q x0 p x1 B"
 DVE_EVAC = 1
 
 
@@ -48,18 +55,21 @@ def tile_extendeddmdkoopmancrossmoment_w8_kernel(tc, x, y_bytes, y_scale, w_word
             return psum.tile([P, BANK], F32, name="bank")
 
         ident = kept("ident", [P, P], F32)
-        ysc_col = kept("ysc_col", [P, 8], F32)
+        ysc_col = kept("ysc_col", [P, 2, 8], F32)
         ysc_all = kept("ysc_all", [P, D], F32)
         b_rows = kept("b_rows", [8, P], BF16)
         b_pad = kept("b_pad", [P, P], F32)
         b_col = kept("b_col", [P, FT], F32)
+        q_f32 = kept("q_f32", [P, 8], F32)
+        q_all = kept("q_all", [P, T], F32)
+        q_bc = kept("q_bc", [P, T], BF16)
         b_all = kept("b_all", [P, F], BF16)
         wt = {"x": kept("p_col", [P, HALVES, 16], BF16), "y": kept("q_col", [P, HALVES, 16], BF16)}
         w_codes = [kept("w_codes%d" % g, [P, F], U32) for g in range(2)]
         w_scale = kept("w_scale", [P, 2 * F], U8)
         y_raw = {(h, v): kept("y_raw%d%d" % (h, v), [P, 2 * D], U8) for h in range(2) for v in range(2)}
         rows = {(s, h, u): kept("rows_%s%d%d" % (s, h, u), [P, D // 2], F32) for s in "xy" for h in range(2) for u in range(4)}
-        turned = {(s, h): kept("turned_%s%d" % (s, h), [P, 2 * BANK * 2], F32) for s in "xy" for h in range(2)}
+        turned = {(s, h, g): kept("turned_%s%d%d" % (s, h, g), [P, 2 * BANK], F32) for s in "xy" for h in range(2) for g in range(2)}
         in_codes = {(s, h, g): kept("in_codes_%s%d%d" % (s, h, g), [P, BANK], U32) for s in "xy" for h in range(2) for g in range(2)}
         in_scale = {(s, h, g): kept("in_scale_%s%d%d" % (s, h, g), [P, BANK], U8) for s in "xy" for h in range(2) for g in range(2)}
         fy = {(h, c): kept("fy%d%d" % (h, c), [P, BANK * PACK], BF16) for h in range(2) for c in range(2)}
@@ -72,17 +82,18 @@ def tile_extendeddmdkoopmancrossmoment_w8_kernel(tc, x, y_bytes, y_scale, w_word
         x_v = x.rearrange("(h m u) d -> h u m d", h=2, u=4)
         y_v = y_bytes.rearrange("(h m v e) d -> h v m (e d)", h=2, v=2, e=2)
 
-        def load_x(h):
-            for u in range(4):
+        def load_x(h, us):
+            for u in us:
                 nc.sync.dma_start(out=rows["x", h, u][:], in_=x_v[h][u].bitcast(F32))
 
-        def load_y(h):
-            for v in range(2):
+        def load_y(h, vs):
+            for v in vs:
                 nc.sync.dma_start(out=y_raw[h, v][:], in_=y_v[h][v])
 
-        def load_w():
-            for g in range(2):
-                nc.sync.dma_start(out=w_codes[g][:].bitcast(I32), in_=w_words[g].rearrange("p n t -> p (n t)").bitcast(I32))
+        def load_w(g):
+            nc.sync.dma_start(out=w_codes[g][:].bitcast(I32), in_=w_words[g].rearrange("p n t -> p (n t)").bitcast(I32))
+
+        def load_ws():
             for quad in range(4):
                 nc.sync.dma_start(
                     out=w_scale[32 * quad : 32 * quad + 4, :].bitcast(I32).rearrange("r (g n) -> r g n", g=2),
@@ -96,76 +107,103 @@ def tile_extendeddmdkoopmancrossmoment_w8_kernel(tc, x, y_bytes, y_scale, w_word
         make_identity(nc, ident[:])
         for item in LOADS.split():
             if item == "s":
-                nc.sync.dma_start(out=ysc_col[:], in_=y_scale.rearrange("o (m c) -> (o m) c", c=8))
+                nc.sync.dma_start(out=ysc_col[:, :, 0:4], in_=y_scale.rearrange("o (g m c) -> m (o g) c", g=2, c=4))
             if item == "b":
                 nc.sync.dma_start(out=b_rows[:], in_=b.rearrange("(c m) -> c m", m=P))
+            if item == "Q":
+                nc.sync.dma_start(out=q_bc[:], in_=q.partition_broadcast(P))
             if item == "B":
                 nc.sync.dma_start(out=b_all[:], in_=b.partition_broadcast(P))
-            if item == "w":
-                load_w()
+            if item[0] == "w":
+                load_w(int(item[1]))
+            if item == "S":
+                load_ws()
             if item == "p":
                 load_wt("x", p)
             if item == "q":
                 load_wt("y", q)
             if item[0] == "x":
-                load_x(int(item[1]))
+                load_x(int(item[1]), [int(c) for c in item[2:]] or range(4))
             if item[0] == "y":
-                load_y(int(item[1]))
+                load_y(int(item[1]), [int(c) for c in item[2:]] or range(2))
 
         nc.scalar.activation(out=b_pad[:], in_=ident[:], func=TANH)
-        for half in range(2):
-            bank = new_bank()
-            for c in range(4):
-                nc.tensor.transpose(bank[:, c * P : (c + 1) * P], ysc_col[:, 4 * half + c : 4 * half + c + 1].to_broadcast([P, P]), ident[:])
-            dst = ysc_all[:].rearrange("p (m c) -> p m c", c=8)[:, :, 4 * half : 4 * half + 4]
-            src = bank[:].rearrange("p (c m) -> p m c", c=4)
-            if half == 0:
-                nc.scalar.copy(out=dst, in_=src)
-            else:
-                nc.vector.tensor_copy(out=dst, in_=src)
-        nc.scalar.copy(out=b_pad[0:8, :], in_=b_rows[:])
-        bank = new_bank()
-        nc.tensor.transpose(bank[:, 0:P], b_pad[:], ident[:])
-        nc.scalar.copy(out=b_col[:], in_=bank[:, 0:FT])
-
         held = {}
 
-        def prep(stage, s, h, u):
-            if stage == 0 and s == "y":
-                raw = y_raw[h, u // 2][:, (u % 2) * D : (u % 2 + 1) * D]
-                nc.vector.tensor_tensor(out=rows[s, h, u][:].bitcast(BF16), in0=raw.bitcast(FP8), in1=ysc_all[:], op=MULT)
-            if stage == 1:
-                bank = new_bank()
-                held["prep", s, h, u] = bank
-                for g in range(2):
-                    for e in range(2):
-                        k = 2 * g + e
-                        nc.tensor.transpose(bank[:, k * P : (k + 1) * P], rows[s, h, u][:, 256 * g + e : 256 * (g + 1) : 2], ident[:])
-            if stage == 2:
-                dst = turned[s, h][:].rearrange("p (g t e) -> p g t e", g=2, e=2)[:, :, u * P : (u + 1) * P, :]
-                nc.scalar.copy(out=dst, in_=held["prep", s, h, u][:].rearrange("p (g e t) -> p g t e", g=2, e=2))
-            if stage == 3 and u == 3:
-                for g in range(2):
-                    nc.vector.quantize_mx(
-                        out=in_codes[s, h, g][:].bitcast(FP8X4),
-                        scales=in_scale[s, h, g][:],
-                        in_=turned[s, h][:, g * 1024 : (g + 1) * 1024].bitcast(BF16),
-                    )
+        def spread_scale(g):
+            bank = new_bank()
+            for c in range(4):
+                nc.tensor.transpose(bank[:, c * P : (c + 1) * P], ysc_col[:, g, c : c + 1].to_broadcast([P, P]), ident[:])
+            nc.scalar.copy(
+                out=ysc_all[:, g * BANK : (g + 1) * BANK].rearrange("p (m c) -> p m c", c=4),
+                in_=bank[:].rearrange("p (c m) -> p m c", c=4),
+            )
+
+        def bias_col():
+            nc.scalar.copy(out=b_pad[0:8, :], in_=b_rows[:])
+            bank = new_bank()
+            nc.tensor.transpose(bank[:, 0:P], b_pad[:], ident[:])
+            nc.scalar.copy(out=b_col[:], in_=bank[:, 0:FT])
+
+        def spread_q(h):
+            if h == 0:
+                nc.scalar.copy(out=q_f32[:].rearrange("p (h u) -> p h u", h=2), in_=wt["y"][:, :, 0:4])
+            bank = new_bank()
+            for u in range(4):
+                nc.tensor.transpose(bank[:, u * P : (u + 1) * P], q_f32[:, 4 * h + u : 4 * h + u + 1].to_broadcast([P, P]), ident[:])
+            nc.scalar.copy(
+                out=q_all[:, h * BANK : (h + 1) * BANK].rearrange("p (v m e) -> p v m e", v=2, e=2),
+                in_=bank[:].rearrange("p (v e m) -> p v m e", v=2, e=2),
+            )
+
+        def turn_c(units):
+            if not units:
+                return
+            bank = new_bank()
+            for k, (s, f, h, route) in enumerate(units):
+                for v in range(2):
+                    col = (2 * k + v) * P
+                    nc.tensor.transpose(bank[:, col : col + P], held[s, f, h][:].bitcast(F32)[:, v * P : (v + 1) * P], ident[:])
+            s, f, h, route = units[0]
+            n = len(units)
+            dst = fy[h, f // 4][:].bitcast(F32)[:, (f % 4) * 256 : (f % 4 + n) * 256]
+            nc.scalar.copy(
+                out=dst.rearrange("p (k f v) -> p k f v", k=n, v=2),
+                in_=bank[:, 0 : n * 256].rearrange("p (k v f) -> p k f v", k=n, v=2),
+            )
+
+        def scale_y(h, u, lo, hi):
+            raw = y_raw[h, u // 2][:, (u % 2) * D + lo : (u % 2) * D + hi]
+            nc.vector.tensor_tensor(out=rows["y", h, u][:].bitcast(BF16)[:, lo:hi], in0=raw.bitcast(FP8), in1=ysc_all[:, lo:hi], op=MULT)
+
+        def turn(s, h, g, us):
+            bank = new_bank()
+            for k, u in enumerate(us):
+                for e in range(2):
+                    col = (2 * k + e) * P
+                    nc.tensor.transpose(bank[:, col : col + P], rows[s, h, u][:, 256 * g + e : 256 * (g + 1) : 2], ident[:])
+            n = len(us)
+            dst = turned[s, h, g][:, us[0] * 256 : (us[0] + n) * 256].rearrange("p (k t e) -> p k t e", k=n, e=2)
+            nc.scalar.copy(out=dst, in_=bank[:, 0 : n * 256].rearrange("p (k e t) -> p k t e", k=n, e=2))
+
+        def quant_in(s, h, g):
+            nc.vector.quantize_mx(out=in_codes[s, h, g][:].bitcast(FP8X4), scales=in_scale[s, h, g][:], in_=turned[s, h, g][:].bitcast(BF16))
 
         def dest(s, f, h):
             if s == "y":
                 return fy[h, f // 4][:, (f % 4) * BANK : (f % 4 + 1) * BANK]
             return fx[f][:, h * BANK : (h + 1) * BANK]
 
-        def unit(stage, s, f, h, route):
+        def unit(stage, s, f, h, route, passes=(0, 1)):
             key = (s, f, h)
             cols = slice(f * P, (f + 1) * P)
             weight = wt[s][:, h, 0:4].unsqueeze(1).to_broadcast([P, P, PACK])
             if stage == 0:
-                bank = new_bank()
-                held[key] = bank
-                if route == "A":
-                    for g in range(2):
+                if 0 in passes:
+                    held[key] = new_bank()
+                bank = held[key]
+                if route != "B":
+                    for g in passes:
                         nc.tensor.matmul_mx(
                             out=bank[:],
                             lhsT=w_codes[g][:, cols].bitcast(FP8X4),
@@ -192,6 +230,13 @@ def tile_extendeddmdkoopmancrossmoment_w8_kernel(tc, x, y_bytes, y_scale, w_word
                 mid = flow.tile([P, BANK], F32, name="mid")
                 if route == "A":
                     nc.scalar.activation(out=mid[:], in_=held[key][:], func=TANH, bias=b_col[:, f : f + 1])
+                elif route == "C":
+                    nc.scalar.activation(
+                        out=mid[:].rearrange("p (v m e) -> p v m e", v=2, e=2),
+                        in_=held[key][:].rearrange("p (v e m) -> p v m e", v=2, e=2),
+                        func=TANH,
+                        bias=b_col[:, f : f + 1],
+                    )
                 else:
                     nc.vector.tensor_tensor(
                         out=mid[:].rearrange("p (f u) -> p f u", u=4),
@@ -201,7 +246,19 @@ def tile_extendeddmdkoopmancrossmoment_w8_kernel(tc, x, y_bytes, y_scale, w_word
                     )
                 held[key] = mid
             if stage == 2:
-                if route == "A":
+                if route == "C":
+                    scaled = flow.tile([P, BANK], BF16, name="scaled")
+                    if QDMA:
+                        nc.vector.tensor_tensor(
+                            out=scaled[:].rearrange("p (v m e) -> p v m e", v=2, e=2),
+                            in0=held[key][:].rearrange("p (v m e) -> p v m e", v=2, e=2),
+                            in1=q_bc[:, h * BANK : (h + 1) * BANK].rearrange("p (m v e) -> p v m e", v=2, e=2),
+                            op=MULT,
+                        )
+                    else:
+                        nc.vector.tensor_tensor(out=scaled[:], in0=held[key][:], in1=q_all[:, h * BANK : (h + 1) * BANK], op=MULT)
+                    held[key] = scaled
+                elif route == "A":
                     bank = new_bank()
                     for u in range(4):
                         nc.tensor.transpose(bank[:, u * P : (u + 1) * P], held[key][:, u * P : (u + 1) * P], ident[:])
@@ -210,19 +267,22 @@ def tile_extendeddmdkoopmancrossmoment_w8_kernel(tc, x, y_bytes, y_scale, w_word
                     act = flow.tile([P, BANK], F32, name="act")
                     nc.scalar.activation(out=act[:], in_=held[key][:], func=TANH)
                     held[key] = act[:].rearrange("p (f u) -> p f u", u=4)
-            if stage == 3:
+            if stage == 3 and route != "C":
                 nc.vector.tensor_tensor(out=dest(s, f, h).rearrange("p (f u) -> p f u", u=4), in0=held[key], in1=weight, op=MULT)
             if stage == 4:
                 if s == "y" and f % 4 == 3:
                     k = (h, f // 4)
                     nc.vector.quantize_mx(out=fy_codes[k][:].bitcast(FP8X4), scales=fy_scale[k][:], in_=fy[k][:])
-                if s == "x" and h == 1:
+                if s == "x" and f >= FT - SPLIT:
+                    nc.vector.quantize_mx(out=fx_codes[f][:, h * P : (h + 1) * P].bitcast(FP8X4), scales=fx_scale[f][:, h * P : (h + 1) * P], in_=fx[f][:, h * BANK : (h + 1) * BANK])
+                elif s == "x" and h == 1:
                     nc.vector.quantize_mx(out=fx_codes[f][:].bitcast(FP8X4), scales=fx_scale[f][:], in_=fx[f][:])
-            if stage == 5 and s == "x" and h == 1:
+            if stage == 5 and s == "x" and (h == 1 or f >= FT - SPLIT):
                 for c in range(2):
-                    bank = new_bank()
-                    held[key, c] = bank
-                    for hh in range(2):
+                    if h == 0 or f < FT - SPLIT:
+                        held["out", f, c] = new_bank()
+                    bank = held["out", f, c]
+                    for hh in (range(2) if f < FT - SPLIT else [h]):
                         hs = slice(hh * P, (hh + 1) * P)
                         nc.tensor.matmul_mx(
                             out=bank[:],
@@ -237,9 +297,9 @@ def tile_extendeddmdkoopmancrossmoment_w8_kernel(tc, x, y_bytes, y_scale, w_word
                 for c in range(2):
                     res = flow.tile([P, BANK], F32, name="res", bufs=8)
                     if c == 1 and f >= FT - DVE_EVAC:
-                        nc.vector.tensor_scalar(out=res[:], in0=held[key, c][:], scalar1=1.0 / DIV, scalar2=None, op0=MULT)
+                        nc.vector.tensor_scalar(out=res[:], in0=held["out", f, c][:], scalar1=1.0 / DIV, scalar2=None, op0=MULT)
                     else:
-                        nc.scalar.activation(out=res[:], in_=held[key, c][:], func=COPY, scale=1.0 / DIV)
+                        nc.scalar.activation(out=res[:], in_=held["out", f, c][:], func=COPY, scale=1.0 / DIV)
                     nc.sync.dma_start(out=out[cols, c * BANK : (c + 1) * BANK], in_=res[:])
 
         ticks = []
@@ -247,35 +307,65 @@ def tile_extendeddmdkoopmancrossmoment_w8_kernel(tc, x, y_bytes, y_scale, w_word
             ticks.append([(word[k], int(word[k + 1]), int(word[k + 2]), word[k + 3]) for k in range(0, len(word), 4)])
         def at(k):
             return ticks[k] if 0 <= k < len(ticks) else []
-        def preps(k):
-            return [(s, h, u) for (s, h), t0 in PREP.items() for u in range(4) if t0[u] == k]
-        for k in range(-8, len(ticks) + 3):
+        spread_scale(0)
+        spread_scale(1)
+        bias_col()
+        for g in range(2):
+            for v in range(2):
+                for u in (2 * v, 2 * v + 1):
+                    scale_y(0, u, g * BANK, (g + 1) * BANK)
+                    if (g, u) == (1, QAT):
+                        quant_in("y", 0, 0)
+                if g == 1 and v == 1:
+                    turn("y", 0, g, [2])
+                    turn("y", 0, g, [3])
+                else:
+                    turn("y", 0, g, [2 * v, 2 * v + 1])
+        early = [un for k in range(EARLY) for un in at(k)]
+        for un in early:
+            unit(0, *un, passes=(0,))
+        for u in range(YHEAD):
+            scale_y(1, u, 0, D)
+        quant_in("y", 0, 1)
+        banks = {k: [] for k in range(-1, 20)}
+        for s, h in TURN:
+            for n in range(4):
+                banks[TURN[s, h][n]].append((s, h, n // 2, n % 2))
+        for k in range(len(ticks) + 3):
             for un in at(k):
-                unit(0, *un)
-            for un in at(k - S2LAG):
+                unit(0, *un, passes=(1,) if un in early else (0, 1))
+            if k >= len(ticks):
+                for un in at(k - 1):
+                    if un[3] == "A":
+                        unit(2, *un)
+            for un in at(k - 3):
                 unit(5, *un)
             for un in at(k - 1):
-                if un[3] == "B":
+                if un[3] in "BC":
                     unit(2, *un)
             for un in at(k):
                 unit(1, *un)
-            for un in at(k - S2LAG):
+            for un in at(k - 3):
                 unit(6, *un)
-            if S2LAG == 3:
-                for un in at(k - 2):
+            for un in at(k - 2):
+                if un[0] == "x":
                     unit(4, *un)
-            for pr in preps(k - 1):
-                prep(3, *pr)
-            for pr in preps(k + 1):
-                prep(0, *pr)
+            for un in at(k - 3):
+                if un[0] == "y":
+                    unit(4, *un)
+            for s, h, g, v in banks[k - 1]:
+                if v == 1:
+                    quant_in(s, h, g)
+            for u in range(YHEAD, 4):
+                if YMUL[u] == k:
+                    scale_y(1, u, 0, D)
+            if QDMA == 0 and k in QSP:
+                spread_q(QSP.index(k))
+            turn_c([un for un in at(k - 2) if un[3] == "C"])
             for un in at(k - 1):
-                if un[3] == "A":
+                if un[3] == "A" and k < len(ticks):
                     unit(2, *un)
-            for pr in preps(k):
-                prep(1, *pr)
-                prep(2, *pr)
+            for s, h, g, v in banks[k]:
+                turn(s, h, g, [2 * v, 2 * v + 1])
             for un in at(k - 1):
                 unit(3, *un)
-            if S2LAG == 2:
-                for un in at(k - 1):
-                    unit(4, *un)

@@ -31,12 +31,12 @@ TURN = {('y', 1): (1, 1, 2, 2), ('x', 0): (0, 0, 3, 3), ('x', 1): (4, 4, 5, 5)}
 YMUL = (0, 0, 0, 0)
 YHEAD = 1
 SPLIT = 0
-QDMA = 1
-QSP = (0, 2)
+ROWS0 = (0,4)
+ROWS1 = ((5,),(1,),())
 QAT = 3
 EARLY = 2
 S2LAG = 3
-LOADS = "s b y0 w0 y1 S w1 Q q x0 p x1 B"
+LOADS = "s y00 v y01 w0 y1 S w1 x0 x1"
 DVE_EVAC = 1
 
 
@@ -57,14 +57,11 @@ def tile_extendeddmdkoopmancrossmoment_w8_kernel(tc, x, y_bytes, y_scale, w_word
         ident = kept("ident", [P, P], F32)
         ysc_col = kept("ysc_col", [P, 2, 8], F32)
         ysc_all = kept("ysc_all", [P, D], F32)
-        b_rows = kept("b_rows", [8, P], BF16)
-        b_pad = kept("b_pad", [P, P], F32)
-        b_col = kept("b_col", [P, FT], F32)
-        q_f32 = kept("q_f32", [P, 8], F32)
-        q_all = kept("q_all", [P, T], F32)
-        q_bc = kept("q_bc", [P, T], BF16)
+        ident_bf = kept("ident_bf", [P, P], BF16)
+        vecs = kept("vecs", [P, BANK], BF16)
+        cols = kept("cols", [P, 24], F32)
+        q_all = kept("q_all", [P, T], BF16)
         b_all = kept("b_all", [P, F], BF16)
-        wt = {"x": kept("p_col", [P, HALVES, 16], BF16), "y": kept("q_col", [P, HALVES, 16], BF16)}
         w_codes = [kept("w_codes%d" % g, [P, F], U32) for g in range(2)]
         w_scale = kept("w_scale", [P, 2 * F], U8)
         y_raw = {(h, v): kept("y_raw%d%d" % (h, v), [P, 2 * D], U8) for h in range(2) for v in range(2)}
@@ -100,34 +97,26 @@ def tile_extendeddmdkoopmancrossmoment_w8_kernel(tc, x, y_bytes, y_scale, w_word
                     in_=w_scales[:, 4 * quad : 4 * quad + 4, :].bitcast(I32).rearrange("g r n -> r g n"),
                 )
 
-        def load_wt(s, vec):
-            nc.sync.dma_start(out=wt[s][:, :, 0:4], in_=vec.rearrange("(h m u) -> m h u", h=2, u=4))
 
+        nc.vector.memset(vecs[:].bitcast(I32), 0)
         nc.vector.memset(w_scale[:].bitcast(I32), 0)
         make_identity(nc, ident[:])
         for item in LOADS.split():
             if item == "s":
                 nc.sync.dma_start(out=ysc_col[:, :, 0:4], in_=y_scale.rearrange("o (g m c) -> m (o g) c", g=2, c=4))
-            if item == "b":
-                nc.sync.dma_start(out=b_rows[:], in_=b.rearrange("(c m) -> c m", m=P))
-            if item == "Q":
-                nc.sync.dma_start(out=q_bc[:], in_=q.partition_broadcast(P))
-            if item == "B":
-                nc.sync.dma_start(out=b_all[:], in_=b.partition_broadcast(P))
+            if item == "v":
+                for r, vec in enumerate((q, p, b)):
+                    nc.sync.dma_start(out=vecs[2 * r : 2 * r + 2, :], in_=vec.rearrange("(h n) -> h n", h=2))
             if item[0] == "w":
                 load_w(int(item[1]))
             if item == "S":
                 load_ws()
-            if item == "p":
-                load_wt("x", p)
-            if item == "q":
-                load_wt("y", q)
             if item[0] == "x":
                 load_x(int(item[1]), [int(c) for c in item[2:]] or range(4))
             if item[0] == "y":
                 load_y(int(item[1]), [int(c) for c in item[2:]] or range(2))
 
-        nc.scalar.activation(out=b_pad[:], in_=ident[:], func=TANH)
+        nc.scalar.activation(out=ident_bf[:], in_=ident[:], func=TANH, scale=100.0)
         held = {}
 
         def spread_scale(g):
@@ -139,22 +128,29 @@ def tile_extendeddmdkoopmancrossmoment_w8_kernel(tc, x, y_bytes, y_scale, w_word
                 in_=bank[:].rearrange("p (c m) -> p m c", c=4),
             )
 
-        def bias_col():
-            nc.scalar.copy(out=b_pad[0:8, :], in_=b_rows[:])
-            bank = new_bank()
-            nc.tensor.transpose(bank[:, 0:P], b_pad[:], ident[:])
-            nc.scalar.copy(out=b_col[:], in_=bank[:, 0:FT])
-
-        def spread_q(h):
-            if h == 0:
-                nc.scalar.copy(out=q_f32[:].rearrange("p (h u) -> p h u", h=2), in_=wt["y"][:, :, 0:4])
+        def columns():
             bank = new_bank()
             for u in range(4):
-                nc.tensor.transpose(bank[:, u * P : (u + 1) * P], q_f32[:, 4 * h + u : 4 * h + u + 1].to_broadcast([P, P]), ident[:])
-            nc.scalar.copy(
-                out=q_all[:, h * BANK : (h + 1) * BANK].rearrange("p (v m e) -> p v m e", v=2, e=2),
-                in_=bank[:].rearrange("p (v e m) -> p v m e", v=2, e=2),
-            )
+                nc.tensor.matmul(bank[:, 4 * u : 4 * u + 4], vecs[:, u::4], ident_bf[:, 0:4], start=True, stop=True)
+            for c in range(4):
+                nc.tensor.matmul(bank[:, 16 + 2 * c : 18 + 2 * c], vecs[:, c * P : (c + 1) * P], ident_bf[:, 4:6], start=True, stop=True)
+            nc.scalar.copy(out=cols[:, 0:16].rearrange("p (r u) -> p r u", u=4), in_=bank[:, 0:16].rearrange("p (u r) -> p r u", u=4))
+            nc.scalar.copy(out=cols[:, 16:24].rearrange("p (g c) -> p g c", g=2), in_=bank[:, 16:24].rearrange("p (c g) -> p g c", g=2))
+
+        def spread_row(r):
+            bank = new_bank()
+            nc.tensor.matmul(bank[:], ident_bf[:, r : r + 1].to_broadcast([P, P]), vecs[:], start=True, stop=True)
+            held["row", r] = bank
+
+        def keep_row(r):
+            bank = held["row", r]
+            if r < 2:
+                nc.scalar.copy(
+                    out=q_all[:, r * BANK : (r + 1) * BANK].rearrange("p (v m e) -> p v m e", v=2, e=2),
+                    in_=bank[:].rearrange("p (m v e) -> p v m e", v=2, e=2),
+                )
+            else:
+                nc.scalar.copy(out=b_all[:, (r - 4) * BANK : (r - 3) * BANK], in_=bank[:])
 
         def turn_c(units):
             if not units:
@@ -196,8 +192,9 @@ def tile_extendeddmdkoopmancrossmoment_w8_kernel(tc, x, y_bytes, y_scale, w_word
 
         def unit(stage, s, f, h, route, passes=(0, 1)):
             key = (s, f, h)
-            cols = slice(f * P, (f + 1) * P)
-            weight = wt[s][:, h, 0:4].unsqueeze(1).to_broadcast([P, P, PACK])
+            fs = slice(f * P, (f + 1) * P)
+            first = 4 * (h + (2 if s == "x" else 0))
+            weight = cols[:, first : first + 4].unsqueeze(1).to_broadcast([P, P, PACK])
             if stage == 0:
                 if 0 in passes:
                     held[key] = new_bank()
@@ -206,7 +203,7 @@ def tile_extendeddmdkoopmancrossmoment_w8_kernel(tc, x, y_bytes, y_scale, w_word
                     for g in passes:
                         nc.tensor.matmul_mx(
                             out=bank[:],
-                            lhsT=w_codes[g][:, cols].bitcast(FP8X4),
+                            lhsT=w_codes[g][:, fs].bitcast(FP8X4),
                             lhsT_scale=w_scale[:, g * F + f * P : g * F + (f + 1) * P],
                             rhs=in_codes[s, h, g][:].bitcast(FP8X4),
                             rhs_scale=in_scale[s, h, g][:],
@@ -221,7 +218,7 @@ def tile_extendeddmdkoopmancrossmoment_w8_kernel(tc, x, y_bytes, y_scale, w_word
                                 out=bank[:, us],
                                 lhsT=in_codes[s, h, g][:, us].bitcast(FP8X4),
                                 lhsT_scale=in_scale[s, h, g][:, us],
-                                rhs=w_codes[g][:, cols].bitcast(FP8X4),
+                                rhs=w_codes[g][:, fs].bitcast(FP8X4),
                                 rhs_scale=w_scale[:, g * F + f * P : g * F + (f + 1) * P],
                                 start=(g == 0),
                                 stop=(g == 1),
@@ -229,34 +226,26 @@ def tile_extendeddmdkoopmancrossmoment_w8_kernel(tc, x, y_bytes, y_scale, w_word
             if stage == 1:
                 mid = flow.tile([P, BANK], F32, name="mid")
                 if route == "A":
-                    nc.scalar.activation(out=mid[:], in_=held[key][:], func=TANH, bias=b_col[:, f : f + 1])
+                    nc.scalar.activation(out=mid[:], in_=held[key][:], func=TANH, bias=cols[:, 16 + f : 17 + f])
                 elif route == "C":
                     nc.scalar.activation(
                         out=mid[:].rearrange("p (v m e) -> p v m e", v=2, e=2),
                         in_=held[key][:].rearrange("p (v e m) -> p v m e", v=2, e=2),
                         func=TANH,
-                        bias=b_col[:, f : f + 1],
+                        bias=cols[:, 16 + f : 17 + f],
                     )
                 else:
                     nc.vector.tensor_tensor(
                         out=mid[:].rearrange("p (f u) -> p f u", u=4),
                         in0=held[key][:].rearrange("p (u f) -> p f u", u=4),
-                        in1=b_all[:, cols].unsqueeze(2).to_broadcast([P, P, PACK]),
+                        in1=b_all[:, fs].unsqueeze(2).to_broadcast([P, P, PACK]),
                         op=ADD,
                     )
                 held[key] = mid
             if stage == 2:
                 if route == "C":
                     scaled = flow.tile([P, BANK], BF16, name="scaled")
-                    if QDMA:
-                        nc.vector.tensor_tensor(
-                            out=scaled[:].rearrange("p (v m e) -> p v m e", v=2, e=2),
-                            in0=held[key][:].rearrange("p (v m e) -> p v m e", v=2, e=2),
-                            in1=q_bc[:, h * BANK : (h + 1) * BANK].rearrange("p (m v e) -> p v m e", v=2, e=2),
-                            op=MULT,
-                        )
-                    else:
-                        nc.vector.tensor_tensor(out=scaled[:], in0=held[key][:], in1=q_all[:, h * BANK : (h + 1) * BANK], op=MULT)
+                    nc.vector.tensor_tensor(out=scaled[:], in0=held[key][:], in1=q_all[:, h * BANK : (h + 1) * BANK], op=MULT)
                     held[key] = scaled
                 elif route == "A":
                     bank = new_bank()
@@ -300,7 +289,7 @@ def tile_extendeddmdkoopmancrossmoment_w8_kernel(tc, x, y_bytes, y_scale, w_word
                         nc.vector.tensor_scalar(out=res[:], in0=held["out", f, c][:], scalar1=1.0 / DIV, scalar2=None, op0=MULT)
                     else:
                         nc.scalar.activation(out=res[:], in_=held["out", f, c][:], func=COPY, scale=1.0 / DIV)
-                    nc.sync.dma_start(out=out[cols, c * BANK : (c + 1) * BANK], in_=res[:])
+                    nc.sync.dma_start(out=out[fs, c * BANK : (c + 1) * BANK], in_=res[:])
 
         ticks = []
         for word in PLAN.split():
@@ -309,7 +298,11 @@ def tile_extendeddmdkoopmancrossmoment_w8_kernel(tc, x, y_bytes, y_scale, w_word
             return ticks[k] if 0 <= k < len(ticks) else []
         spread_scale(0)
         spread_scale(1)
-        bias_col()
+        columns()
+        for r in ROWS0:
+            spread_row(r)
+        for r in ROWS0:
+            keep_row(r)
         for g in range(2):
             for v in range(2):
                 for u in (2 * v, 2 * v + 1):
@@ -321,6 +314,9 @@ def tile_extendeddmdkoopmancrossmoment_w8_kernel(tc, x, y_bytes, y_scale, w_word
                     turn("y", 0, g, [3])
                 else:
                     turn("y", 0, g, [2 * v, 2 * v + 1])
+                    for r in ROWS1[2 * g + v]:
+                        spread_row(r)
+                        keep_row(r)
         early = [un for k in range(EARLY) for un in at(k)]
         for un in early:
             unit(0, *un, passes=(0,))
@@ -359,8 +355,6 @@ def tile_extendeddmdkoopmancrossmoment_w8_kernel(tc, x, y_bytes, y_scale, w_word
             for u in range(YHEAD, 4):
                 if YMUL[u] == k:
                     scale_y(1, u, 0, D)
-            if QDMA == 0 and k in QSP:
-                spread_q(QSP.index(k))
             turn_c([un for un in at(k - 2) if un[3] == "C"])
             for un in at(k - 1):
                 if un[3] == "A" and k < len(ticks):

from contextlib import ExitStack

import concourse.mybir as mybir
from concourse.masks import make_identity

T, D, F = 1024, 1024, 1024
DIV = 32.0
FLOPS = 3 * 2 * T * D * F

F32 = mybir.dt.float32
BF16 = mybir.dt.bfloat16
U32 = mybir.dt.uint32
I32 = mybir.dt.int32
U8 = mybir.dt.uint8
FP8 = mybir.dt.float8_e4m3fn
FP8X4 = mybir.dt.float8_e4m3fn_x4
MULT = mybir.AluOpType.mult
ADD = mybir.AluOpType.add
TANH = mybir.ActivationFunctionType.Tanh
COPY = mybir.ActivationFunctionType.Copy

P = 128
PACK = 4
BANK = 512
HALVES = 2
FT = F // P

NFILL = 0
PLAN = "y00Cy10C y20Cy30C y40By50C y60By70C y01By11C y21By31C y41By51C y61Cy71C x00Ax01A x10Bx11A x20Bx21A x30Bx31B x40Bx41B x50Bx51B x60Bx61A x70Ax71A"
TURN = {('y', 1): (1, 1, 2, 2), ('x', 0): (0, 0, 3, 3), ('x', 1): (4, 4, 5, 5)}
YMUL = (0, 0, 0, 0)
YHEAD = 1
SPLIT = 0
ROWS0 = (0,4)
ROWS1 = ((5,),(1,),())
QAT = 3
EARLY = 2
S2LAG = 3
LOADS = "s y00 v y01 w0 y1 S w1 x0 x1"
DVE_EVAC = 1


def tile_extendeddmdkoopmancrossmoment_w8_kernel(tc, x, y_bytes, y_scale, w_words, w_scales, b, p, q, out):
    nc = tc.nc
    with ExitStack() as ctx:
        keep = ctx.enter_context(tc.tile_pool(name="keep", bufs=1))
        flow = ctx.enter_context(tc.tile_pool(name="flow", bufs=4))
        psum = ctx.enter_context(tc.psum_pool(name="psum", bufs=8))
        ctx.enter_context(tc.manual_schedule())

        def kept(name, shape, dtype):
            return keep.tile(shape, dtype, name=name, align_bytes=64)

        def new_bank():
            return psum.tile([P, BANK], F32, name="bank")

        ident = kept("ident", [P, P], F32)
        ysc_col = kept("ysc_col", [P, 2, 8], F32)
        ysc_all = kept("ysc_all", [P, D], F32)
        ident_bf = kept("ident_bf", [P, P], BF16)
        vecs = kept("vecs", [P, BANK], BF16)
        cols = kept("cols", [P, 24], F32)
        q_all = kept("q_all", [P, T], BF16)
        b_all = kept("b_all", [P, F], BF16)
        w_codes = [kept("w_codes%d" % g, [P, F], U32) for g in range(2)]
        w_scale = kept("w_scale", [P, 2 * F], U8)
        y_raw = {(h, v): kept("y_raw%d%d" % (h, v), [P, 2 * D], U8) for h in range(2) for v in range(2)}
        rows = {(s, h, u): kept("rows_%s%d%d" % (s, h, u), [P, D // 2], F32) for s in "xy" for h in range(2) for u in range(4)}
        turned = {(s, h, g): kept("turned_%s%d%d" % (s, h, g), [P, 2 * BANK], F32) for s in "xy" for h in range(2) for g in range(2)}
        in_codes = {(s, h, g): kept("in_codes_%s%d%d" % (s, h, g), [P, BANK], U32) for s in "xy" for h in range(2) for g in range(2)}
        in_scale = {(s, h, g): kept("in_scale_%s%d%d" % (s, h, g), [P, BANK], U8) for s in "xy" for h in range(2) for g in range(2)}
        fy = {(h, c): kept("fy%d%d" % (h, c), [P, BANK * PACK], BF16) for h in range(2) for c in range(2)}
        fy_codes = {k: kept("fy_codes%d%d" % k, [P, BANK], U32) for k in fy}
        fy_scale = {k: kept("fy_scale%d%d" % k, [P, BANK], U8) for k in fy}
        fx = {i: kept("fx%d" % i, [P, 2 * P * PACK], BF16) for i in range(FT)}
        fx_codes = {i: kept("fx_codes%d" % i, [P, 2 * P], U32) for i in range(FT)}
        fx_scale = {i: kept("fx_scale%d" % i, [P, 2 * P], U8) for i in range(FT)}

        x_v = x.rearrange("(h m u) d -> h u m d", h=2, u=4)
        y_v = y_bytes.rearrange("(h m v e) d -> h v m (e d)", h=2, v=2, e=2)

        def load_x(h, us):
            for u in us:
                nc.sync.dma_start(out=rows["x", h, u][:], in_=x_v[h][u].bitcast(F32))

        def load_y(h, vs):
            for v in vs:
                nc.sync.dma_start(out=y_raw[h, v][:], in_=y_v[h][v])

        def load_w(g):
            nc.sync.dma_start(out=w_codes[g][:].bitcast(I32), in_=w_words[g].rearrange("p n t -> p (n t)").bitcast(I32))

        def load_ws():
            for quad in range(4):
                nc.sync.dma_start(
                    out=w_scale[32 * quad : 32 * quad + 4, :].bitcast(I32).rearrange("r (g n) -> r g n", g=2),
                    in_=w_scales[:, 4 * quad : 4 * quad + 4, :].bitcast(I32).rearrange("g r n -> r g n"),
                )


        nc.vector.memset(vecs[:].bitcast(I32), 0)
        nc.vector.memset(w_scale[:].bitcast(I32), 0)
        make_identity(nc, ident[:])
        for item in LOADS.split():
            if item == "s":
                nc.sync.dma_start(out=ysc_col[:, :, 0:4], in_=y_scale.rearrange("o (g m c) -> m (o g) c", g=2, c=4))
            if item == "v":
                for r, vec in enumerate((q, p, b)):
                    nc.sync.dma_start(out=vecs[2 * r : 2 * r + 2, :], in_=vec.rearrange("(h n) -> h n", h=2))
            if item[0] == "w":
                load_w(int(item[1]))
            if item == "S":
                load_ws()
            if item[0] == "x":
                load_x(int(item[1]), [int(c) for c in item[2:]] or range(4))
            if item[0] == "y":
                load_y(int(item[1]), [int(c) for c in item[2:]] or range(2))

        nc.scalar.activation(out=ident_bf[:], in_=ident[:], func=TANH, scale=100.0)
        held = {}

        def spread_scale(g):
            bank = new_bank()
            for c in range(4):
                nc.tensor.transpose(bank[:, c * P : (c + 1) * P], ysc_col[:, g, c : c + 1].to_broadcast([P, P]), ident[:])
            nc.scalar.copy(
                out=ysc_all[:, g * BANK : (g + 1) * BANK].rearrange("p (m c) -> p m c", c=4),
                in_=bank[:].rearrange("p (c m) -> p m c", c=4),
            )

        def columns():
            bank = new_bank()
            for u in range(4):
                nc.tensor.matmul(bank[:, 4 * u : 4 * u + 4], vecs[:, u::4], ident_bf[:, 0:4], start=True, stop=True)
            for c in range(4):
                nc.tensor.matmul(bank[:, 16 + 2 * c : 18 + 2 * c], vecs[:, c * P : (c + 1) * P], ident_bf[:, 4:6], start=True, stop=True)
            nc.scalar.copy(out=cols[:, 0:16].rearrange("p (r u) -> p r u", u=4), in_=bank[:, 0:16].rearrange("p (u r) -> p r u", u=4))
            nc.scalar.copy(out=cols[:, 16:24].rearrange("p (g c) -> p g c", g=2), in_=bank[:, 16:24].rearrange("p (c g) -> p g c", g=2))

        def spread_row(r):
            bank = new_bank()
            nc.tensor.matmul(bank[:], ident_bf[:, r : r + 1].to_broadcast([P, P]), vecs[:], start=True, stop=True)
            held["row", r] = bank

        def keep_row(r):
            bank = held["row", r]
            if r < 2:
                nc.scalar.copy(
                    out=q_all[:, r * BANK : (r + 1) * BANK].rearrange("p (v m e) -> p v m e", v=2, e=2),
                    in_=bank[:].rearrange("p (m v e) -> p v m e", v=2, e=2),
                )
            else:
                nc.scalar.copy(out=b_all[:, (r - 4) * BANK : (r - 3) * BANK], in_=bank[:])

        def turn_c(units):
            if not units:
                return
            bank = new_bank()
            for k, (s, f, h, route) in enumerate(units):
                for v in range(2):
                    col = (2 * k + v) * P
                    nc.tensor.transpose(bank[:, col : col + P], held[s, f, h][:].bitcast(F32)[:, v * P : (v + 1) * P], ident[:])
            s, f, h, route = units[0]
            n = len(units)
            dst = fy[h, f // 4][:].bitcast(F32)[:, (f % 4) * 256 : (f % 4 + n) * 256]
            nc.scalar.copy(
                out=dst.rearrange("p (k f v) -> p k f v", k=n, v=2),
                in_=bank[:, 0 : n * 256].rearrange("p (k v f) -> p k f v", k=n, v=2),
            )

        def scale_y(h, u, lo, hi):
            raw = y_raw[h, u // 2][:, (u % 2) * D + lo : (u % 2) * D + hi]
            nc.vector.tensor_tensor(out=rows["y", h, u][:].bitcast(BF16)[:, lo:hi], in0=raw.bitcast(FP8), in1=ysc_all[:, lo:hi], op=MULT)

        def turn(s, h, g, us):
            bank = new_bank()
            for k, u in enumerate(us):
                for e in range(2):
                    col = (2 * k + e) * P
                    nc.tensor.transpose(bank[:, col : col + P], rows[s, h, u][:, 256 * g + e : 256 * (g + 1) : 2], ident[:])
            n = len(us)
            dst = turned[s, h, g][:, us[0] * 256 : (us[0] + n) * 256].rearrange("p (k t e) -> p k t e", k=n, e=2)
            nc.scalar.copy(out=dst, in_=bank[:, 0 : n * 256].rearrange("p (k e t) -> p k t e", k=n, e=2))

        def quant_in(s, h, g):
            nc.vector.quantize_mx(out=in_codes[s, h, g][:].bitcast(FP8X4), scales=in_scale[s, h, g][:], in_=turned[s, h, g][:].bitcast(BF16))

        def dest(s, f, h):
            if s == "y":
                return fy[h, f // 4][:, (f % 4) * BANK : (f % 4 + 1) * BANK]
            return fx[f][:, h * BANK : (h + 1) * BANK]

        def unit(stage, s, f, h, route, passes=(0, 1)):
            key = (s, f, h)
            fs = slice(f * P, (f + 1) * P)
            first = 4 * (h + (2 if s == "x" else 0))
            weight = cols[:, first : first + 4].unsqueeze(1).to_broadcast([P, P, PACK])
            if stage == 0:
                if 0 in passes:
                    held[key] = new_bank()
                bank = held[key]
                if route != "B":
                    for g in passes:
                        nc.tensor.matmul_mx(
                            out=bank[:],
                            lhsT=w_codes[g][:, fs].bitcast(FP8X4),
                            lhsT_scale=w_scale[:, g * F + f * P : g * F + (f + 1) * P],
                            rhs=in_codes[s, h, g][:].bitcast(FP8X4),
                            rhs_scale=in_scale[s, h, g][:],
                            start=(g == 0),
                            stop=(g == 1),
                        )
                else:
                    for u in range(4):
                        us = slice(u * P, (u + 1) * P)
                        for g in range(2):
                            nc.tensor.matmul_mx(
                                out=bank[:, us],
                                lhsT=in_codes[s, h, g][:, us].bitcast(FP8X4),
                                lhsT_scale=in_scale[s, h, g][:, us],
                                rhs=w_codes[g][:, fs].bitcast(FP8X4),
                                rhs_scale=w_scale[:, g * F + f * P : g * F + (f + 1) * P],
                                start=(g == 0),
                                stop=(g == 1),
                            )
            if stage == 1:
                mid = flow.tile([P, BANK], F32, name="mid")
                if route == "A":
                    nc.scalar.activation(out=mid[:], in_=held[key][:], func=TANH, bias=cols[:, 16 + f : 17 + f])
                elif route == "C":
                    nc.scalar.activation(
                        out=mid[:].rearrange("p (v m e) -> p v m e", v=2, e=2),
                        in_=held[key][:].rearrange("p (v e m) -> p v m e", v=2, e=2),
                        func=TANH,
                        bias=cols[:, 16 + f : 17 + f],
                    )
                else:
                    nc.vector.tensor_tensor(
                        out=mid[:].rearrange("p (f u) -> p f u", u=4),
                        in0=held[key][:].rearrange("p (u f) -> p f u", u=4),
                        in1=b_all[:, fs].unsqueeze(2).to_broadcast([P, P, PACK]),
                        op=ADD,
                    )
                held[key] = mid
            if stage == 2:
                if route == "C":
                    scaled = flow.tile([P, BANK], BF16, name="scaled")
                    nc.vector.tensor_tensor(out=scaled[:], in0=held[key][:], in1=q_all[:, h * BANK : (h + 1) * BANK], op=MULT)
                    held[key] = scaled
                elif route == "A":
                    bank = new_bank()
                    for u in range(4):
                        nc.tensor.transpose(bank[:, u * P : (u + 1) * P], held[key][:, u * P : (u + 1) * P], ident[:])
                    held[key] = bank[:].rearrange("p (u f) -> p f u", u=4)
                else:
                    act = flow.tile([P, BANK], F32, name="act")
                    nc.scalar.activation(out=act[:], in_=held[key][:], func=TANH)
                    held[key] = act[:].rearrange("p (f u) -> p f u", u=4)
            if stage == 3 and route != "C":
                nc.vector.tensor_tensor(out=dest(s, f, h).rearrange("p (f u) -> p f u", u=4), in0=held[key], in1=weight, op=MULT)
            if stage == 4:
                if s == "y" and f % 4 == 3:
                    k = (h, f // 4)
                    nc.vector.quantize_mx(out=fy_codes[k][:].bitcast(FP8X4), scales=fy_scale[k][:], in_=fy[k][:])
                if s == "x" and f >= FT - SPLIT:
                    nc.vector.quantize_mx(out=fx_codes[f][:, h * P : (h + 1) * P].bitcast(FP8X4), scales=fx_scale[f][:, h * P : (h + 1) * P], in_=fx[f][:, h * BANK : (h + 1) * BANK])
                elif s == "x" and h == 1:
                    nc.vector.quantize_mx(out=fx_codes[f][:].bitcast(FP8X4), scales=fx_scale[f][:], in_=fx[f][:])
            if stage == 5 and s == "x" and (h == 1 or f >= FT - SPLIT):
                for c in range(2):
                    if h == 0 or f < FT - SPLIT:
                        held["out", f, c] = new_bank()
                    bank = held["out", f, c]
                    for hh in (range(2) if f < FT - SPLIT else [h]):
                        hs = slice(hh * P, (hh + 1) * P)
                        nc.tensor.matmul_mx(
                            out=bank[:],
                            lhsT=fx_codes[f][:, hs].bitcast(FP8X4),
                            lhsT_scale=fx_scale[f][:, hs],
                            rhs=fy_codes[hh, c][:].bitcast(FP8X4),
                            rhs_scale=fy_scale[hh, c][:],
                            start=(hh == 0),
                            stop=(hh == 1),
                        )
            if stage == 6 and s == "x" and h == 1:
                for c in range(2):
                    res = flow.tile([P, BANK], F32, name="res", bufs=8)
                    if c == 1 and f >= FT - DVE_EVAC:
                        nc.vector.tensor_scalar(out=res[:], in0=held["out", f, c][:], scalar1=1.0 / DIV, scalar2=None, op0=MULT)
                    else:
                        nc.scalar.activation(out=res[:], in_=held["out", f, c][:], func=COPY, scale=1.0 / DIV)
                    nc.sync.dma_start(out=out[fs, c * BANK : (c + 1) * BANK], in_=res[:])

        ticks = []
        for word in PLAN.split():
            ticks.append([(word[k], int(word[k + 1]), int(word[k + 2]), word[k + 3]) for k in range(0, len(word), 4)])
        def at(k):
            return ticks[k] if 0 <= k < len(ticks) else []
        spread_scale(0)
        spread_scale(1)
        columns()
        for r in ROWS0:
            spread_row(r)
        for r in ROWS0:
            keep_row(r)
        for g in range(2):
            for v in range(2):
                for u in (2 * v, 2 * v + 1):
                    scale_y(0, u, g * BANK, (g + 1) * BANK)
                    if (g, u) == (1, QAT):
                        quant_in("y", 0, 0)
                if g == 1 and v == 1:
                    turn("y", 0, g, [2])
                    turn("y", 0, g, [3])
                else:
                    turn("y", 0, g, [2 * v, 2 * v + 1])
                    for r in ROWS1[2 * g + v]:
                        spread_row(r)
                        keep_row(r)
        early = [un for k in range(EARLY) for un in at(k)]
        for un in early:
            unit(0, *un, passes=(0,))
        for u in range(YHEAD):
            scale_y(1, u, 0, D)
        quant_in("y", 0, 1)
        banks = {k: [] for k in range(-1, 20)}
        for s, h in TURN:
            for n in range(4):
                banks[TURN[s, h][n]].append((s, h, n // 2, n % 2))
        for k in range(len(ticks) + 3):
            for un in at(k):
                unit(0, *un, passes=(1,) if un in early else (0, 1))
            if k >= len(ticks):
                for un in at(k - 1):
                    if un[3] == "A":
                        unit(2, *un)
            for un in at(k - 3):
                unit(5, *un)
            for un in at(k - 1):
                if un[3] in "BC":
                    unit(2, *un)
            for un in at(k):
                unit(1, *un)
            for un in at(k - 3):
                unit(6, *un)
            for un in at(k - 2):
                if un[0] == "x":
                    unit(4, *un)
            for un in at(k - 3):
                if un[0] == "y":
                    unit(4, *un)
            for s, h, g, v in banks[k - 1]:
                if v == 1:
                    quant_in(s, h, g)
            for u in range(YHEAD, 4):
                if YMUL[u] == k:
                    scale_y(1, u, 0, D)
            turn_c([un for un in at(k - 2) if un[3] == "C"])
            for un in at(k - 1):
                if un[3] == "A" and k < len(ticks):
                    unit(2, *un)
            for s, h, g, v in banks[k]:
                turn(s, h, g, [2 * v, 2 * v + 1])
            for un in at(k - 1):
                unit(3, *un)
